import numpy as np
import ml_dtypes


def mxq(x, axis, fmt="e4m3"):
    dtype, down = {"e4m3": (ml_dtypes.float8_e4m3fn, 7), "e5m2": (ml_dtypes.float8_e5m2, 14)}[fmt]
    v = np.moveaxis(np.asarray(x, np.float32).astype(ml_dtypes.bfloat16).astype(np.float64), axis, -1)
    blocks = v.reshape(v.shape[:-1] + (-1, 32))
    amax = np.abs(blocks).max(-1, keepdims=True)
    byte = np.maximum(np.where(amax > 0, np.frexp(amax)[1] - 1 + 127, 0) - down, 1)
    scale = np.exp2(byte - 127.0)
    codes = (blocks / scale).astype(np.float32).astype(dtype).astype(np.float64)
    return np.moveaxis((codes * scale).reshape(v.shape), -1, axis)


WIDE = False


def mx_kscale(k):
    if not WIDE:
        return np.ones(k)
    levels = np.array([10, -10, 5, -5, 0])
    if k % 512:
        return np.exp2(np.random.permutation(np.resize(levels, k // 32))).repeat(32)
    a = np.empty((k // 512, 16))
    for p in range(k // 512):
        a[p, :8] = np.random.permutation(np.resize(levels, 8))
        for g in range(8):
            far = levels[np.abs(levels - a[p, g]) >= 10]
            a[p, g + 8] = far[np.random.randint(len(far))]
    return np.exp2(a.ravel()).repeat(32)


def f64(x):
    return np.asarray(x).astype(np.float64)


def striped(idx):
    return np.tile(idx.reshape(-1, 16).T, (8, 1)).astype(np.uint16)


def unstriped(offs):
    return offs[:16].T.reshape(-1).astype(np.int64)


def striped8(idx):
    return np.concatenate([x.reshape(-1, 16).T for x in idx]).astype(np.uint16)


def runs(offs, k):
    lists = np.stack([offs[16 * r : 16 * r + 16].T.reshape(-1) for r in range(8)]).astype(np.int64)
    return lists[np.arange(k) % 512 // 64]


def pack_weight(w):
    k, n = w.shape
    w = f64(np.asarray(w, np.float32).astype(ml_dtypes.bfloat16)).reshape(k // 32, 32, n)
    amax = np.abs(w).max(1)
    byte = np.clip(np.where(amax > 0, np.frexp(amax)[1] - 1 + 127 - 7, 1), 1, 254)
    scaled = (w * np.exp2(127.0 - byte)[:, None, :]).reshape(k, n).astype(np.float32)
    words = np.ascontiguousarray(scaled.reshape(k // 512, 128, 4, n).transpose(0, 1, 3, 2)).astype(ml_dtypes.float8_e4m3fn).view(np.uint8)
    return words, np.ascontiguousarray(byte.astype(np.uint8).reshape(k // 512, 16, n))


def unpack_weight(words, scales):
    g, p, n, _ = words.shape
    vals = np.ascontiguousarray(words).view(ml_dtypes.float8_e4m3fn).astype(np.float64) * np.repeat(np.exp2(scales.astype(np.float64) - 127.0), 8, axis=1)[..., None]
    return vals.transpose(0, 1, 3, 2).reshape(g * 512, n)


K, T, S, H, G = 512, 1024, 256, 512, 2048


def setup_inputs():
    n = np.random.standard_normal
    s = mx_kscale(K)[:, None]
    packed_xT = pack_weight(n((K, T)) * s)
    packed_dT = pack_weight(n((K, G)) / s)
    return {
        "x_words": packed_xT[0],
        "x_scales": packed_xT[1],
        "w1": (n((K, H)) / np.sqrt(K) / s).astype(np.float32),
        "w2": (n((K, H)) / np.sqrt(K) / s).astype(np.float32),
        "gs": (np.random.uniform(0.5, 1.5, (K, 1)) * s).astype(np.float32),
        "d_words": packed_dT[0],
        "d_scales": packed_dT[1],
        "offs": striped(np.random.permutation(T)[:S]),
        "two": striped(np.random.permutation(T)[:S]),
        "n1": striped(np.random.permutation(S)),
        "n2": striped(np.random.permutation(S)),
        "n3": striped(np.random.permutation(S)),
        "k1": striped8(np.random.randint(0, G, (8, H))),
        "n4": striped(np.random.permutation(S)),
        "n5": striped(np.random.permutation(S)),
        "n6": striped(np.random.permutation(S)),
    }


def reference(x_words, x_scales, w1, w2, gs, d_words, d_scales, offs, two, n1, n2, n3, k1, n4, n5, n6):
    d_k1 = unpack_weight(d_words, d_scales)[np.arange(K)[:, None], runs(k1, K)]
    xq = unpack_weight(x_words, x_scales)[:, unstriped(offs)]
    y = mxq(f64(w1), 0, "e4m3").T @ xq
    x_two = unpack_weight(x_words, x_scales)[:, unstriped(two)]
    d = mxq(f64(w2), 0, "e4m3").T @ x_two
    z = f64(gs) * (np.maximum(np.minimum(y - (0.5 * y[:, unstriped(n1)]), d[:, unstriped(n2)]), d[:, unstriped(n3)]))
    h = 0.0625 * ((d_k1.T @ mxq(z, 0, "e4m3")))
    ex = np.exp(0.5 * h)
    return np.log((ex + ex[:, unstriped(n4)]) / (ex[:, unstriped(n5)] + ex[:, unstriped(n6)]))

@@ -1,0 +1,222 @@
+from contextlib import ExitStack
+
+import concourse.mybir as mybir
+
+K, T, S, H, G = 512, 1024, 256, 512, 2048
+FLOPS = 3 * 2 * K * H * S
+
+F32 = mybir.dt.float32
+BF16 = mybir.dt.bfloat16
+I32 = mybir.dt.int32
+U32 = mybir.dt.uint32
+U16 = mybir.dt.uint16
+U8 = mybir.dt.uint8
+FP8X4 = mybir.dt.float8_e4m3fn_x4
+ALU = mybir.AluOpType
+ACT = mybir.ActivationFunctionType
+
+P = 128
+PACK = 4
+HALF = S // 2
+SPARE = 8
+
+
+def tile_picked_twqclampbodds_none_p_kernel(
+    tc, x_words, x_scales, w1, w2, gs, d_words, d_scales, offs, two, n1, n2, n3, k1, n4, n5, n6, out
+):
+    nc = tc.nc
+    with ExitStack() as ctx:
+        keep = ctx.enter_context(tc.tile_pool(name="keep", bufs=1))
+        psum = ctx.enter_context(tc.psum_pool(name="psum", bufs=1))
+
+        def sb(name, shape, dtype, tag=""):
+            return keep.tile(shape, dtype, name=name, align_bytes=64, tag=tag or name)
+
+        def load_list(name, src):
+            t = sb(name, list(src.shape), U16)
+            nc.sync.dma_start(t[:], src)
+            return t
+
+        def half_of(lst, h):
+            return lst[:, h * HALF // 16 : (h + 1) * HALF // 16]
+
+        xs_tab = sb("xs_tab", [P, T], U8)
+        ds_tab = sb("ds_tab", [P, G], U8)
+        ds_placed = sb("ds_placed", [P, H], U8)
+        xw_tab = sb("xw_tab", [P, T], U32)
+        dw_tab = sb("dw_tab", [P, G], U32)
+        ex = [sb("ex%d" % b, [P, S + SPARE], F32) for b in range(4)]
+        y = [sb("y%d" % t, [P, S + SPARE], F32) for t in range(PACK)]
+        d = [sb("d%d" % t, [P, S + SPARE], F32) for t in range(PACK)]
+
+        nc.gpsimd.memset(ds_tab[:].bitcast(I32), 0)
+        nc.gpsimd.memset(ds_placed[:].bitcast(I32), 0)
+        for win in d + y + ex:
+            nc.gpsimd.memset(win[:, S:], 0.0)
+
+        xs_rows = x_scales[0].bitcast(I32)
+        for q in range(4):
+            rows = xs_rows[4 * q : 4 * q + 4, :].rearrange("(a r) c -> a r c", a=1).to_broadcast([8, 4, T // 4])
+            nc.sync.dma_start(xs_tab[32 * q : 32 * q + 32, :].bitcast(I32), rows)
+        two_t = load_list("two_t", two)
+        offs_t = load_list("offs_t", offs)
+
+        def load_w(name, w):
+            rows = w.rearrange("(p j) c -> p j c", j=PACK)
+            parts = []
+            for u in range(2):
+                t = sb("%s_raw%d" % (name, u), [P, 2, H], F32)
+                nc.sync.dma_start(t[:], rows[:, 2 * u : 2 * u + 2, :])
+                parts.append(t)
+            return parts
+
+        w2_raw = load_w("w2", w2)
+        nc.sync.dma_start(xw_tab[:].bitcast(I32), x_words[0].rearrange("p n t -> p (n t)").bitcast(I32))
+        n2_t = load_list("n2_t", n2)
+        w1_raw = load_w("w1", w1)
+        n1_t = load_list("n1_t", n1)
+        n3_t = load_list("n3_t", n3)
+        k1_t = load_list("k1_t", k1)
+        ds_rows = d_scales[0].bitcast(I32)
+        for r in range(2):
+            nc.sync.dma_start(ds_tab[r:P:16, :].bitcast(I32), ds_rows[r:16:2, :])
+        nc.sync.dma_start(dw_tab[:].bitcast(I32), d_words[0].rearrange("p n t -> p (n t)").bitcast(I32))
+        gs4 = sb("gs4", [P, PACK], F32)
+        nc.sync.dma_start(gs4[:], gs.rearrange("(p t) o -> p (t o)", t=PACK))
+        n4_t = load_list("n4_t", n4)
+        n5_t = load_list("n5_t", n5)
+        n6_t = load_list("n6_t", n6)
+
+        def cast_w(engine_copy, wb, raw, u):
+            dst = wb[:].rearrange("p (t m i j) -> p m t i j", t=PACK, i=2, j=PACK)[:, :, :, :, 2 * u : 2 * u + 2]
+            src = raw[:].rearrange("p j (m i t) -> p m t i j", i=2, t=PACK)
+            engine_copy(dst, src)
+
+        def quantise_w(name, wb):
+            codes = sb(name + "_codes", [P, H], U32)
+            scales = sb(name + "_scales", [P, H], U8)
+            for v in range(2):
+                cols = slice(v * 2 * P, (v + 1) * 2 * P)
+                nc.vector.quantize_mx(
+                    out=codes[:, cols].bitcast(FP8X4), scales=scales[:, cols],
+                    in_=wb[:, v * 2 * P * PACK : (v + 1) * 2 * P * PACK])
+            return codes, scales
+
+        def project(name, codes, scales, x_w, x_s):
+            banks = []
+            for t in range(PACK):
+                bank = psum.tile([P, S], F32, name="%s_bank%d" % (name, t))
+                cols = slice(t * P, (t + 1) * P)
+                nc.tensor.matmul_mx(
+                    out=bank[:], lhsT=codes[:, cols].bitcast(FP8X4), lhsT_scale=scales[:, cols],
+                    rhs=x_w[:].bitcast(FP8X4), rhs_scale=x_s[:], start=True, stop=True)
+                banks.append(bank)
+            return banks
+
+        x2_s = sb("x2_s", [P, S], U8)
+        nc.vector.tensor_copy(x2_s[:], xs_tab[:].indirect(two_t[:]))
+        x1_s = sb("x1_s", [P, S], U8)
+        nc.vector.tensor_copy(x1_s[:], xs_tab[:].indirect(offs_t[:]))
+        w2b = sb("w2b", [P, H * PACK], BF16)
+        cast_w(nc.scalar.copy, w2b, w2_raw[0], 0)
+        cast_w(nc.vector.tensor_copy, w2b, w2_raw[1], 1)
+        d_codes, d_sc = quantise_w("d", w2b)
+        x2_w = sb("x2_w", [P, S], U32)
+        nc.vector.tensor_copy(x2_w[:], xw_tab[:].indirect(two_t[:]))
+        d_banks = project("d", d_codes, d_sc, x2_w, x2_s)
+
+        g1 = sb("g1", [P, PACK, S], F32)
+        g2 = sb("g2", [P, PACK, S], F32)
+        for t in range(PACK + 1):
+            if t < PACK:
+                nc.scalar.copy(d[t][:, :S], d_banks[t][:])
+            if t > 0:
+                nc.scalar.activation(g2[:, t - 1, :], d[t - 1][:].indirect(n2_t[:]), ACT.Copy)
+
+        x1_w = sb("x1_w", [P, S], U32)
+        nc.vector.tensor_copy(x1_w[:], xw_tab[:].indirect(offs_t[:]))
+        w1b = sb("w1b", [P, H * PACK], BF16)
+        cast_w(nc.vector.tensor_copy, w1b, w1_raw[0], 0)
+        cast_w(nc.vector.tensor_copy, w1b, w1_raw[1], 1)
+        y_codes, y_sc = quantise_w("y", w1b)
+        y_banks = project("y", y_codes, y_sc, x1_w, x1_s)
+        for t in range(PACK + 1):
+            if t < PACK:
+                nc.scalar.copy(y[t][:, :S], y_banks[t][:])
+            if t > 0:
+                nc.scalar.activation(g1[:, t - 1, :], y[t - 1][:].indirect(n1_t[:]), ACT.Copy, scale=-0.5)
+
+        dg_s = sb("dg_s", [P, H], U8, tag="w1b")
+        nc.vector.tensor_copy(dg_s[:], ds_tab[:].indirect(k1_t[:]))
+        for i in range(4):
+            nc.sync.dma_start(ds_placed[i:P:32, :].bitcast(I32), dg_s[16 * (i // 2) + i % 2 : P : 32, :].bitcast(I32))
+        dg_w = sb("dg_w", [P, H], U32)
+        nc.vector.tensor_copy(dg_w[:], dw_tab[:].indirect(k1_t[:]))
+
+        g3 = [sb("g3_0", [P, PACK, HALF], F32, tag="y_codes"), sb("g3_1", [P, PACK, HALF], F32, tag="y_scales")]
+        for h in range(2):
+            for t in range(PACK):
+                nc.scalar.activation(g3[h][:, t, :], d[t][:].indirect(half_of(n3_t, h)), ACT.Copy)
+
+        a = sb("a", [P, PACK, S], F32, tag="dw_tab")
+        m = sb("m", [P, PACK, S], F32)
+        for t in range(PACK + 1):
+            if t < PACK:
+                nc.vector.tensor_tensor(a[:, t, :], g1[:, t, :], y[t][:, :S], ALU.add)
+            if t > 0:
+                nc.vector.tensor_tensor(m[:, t - 1, :], a[:, t - 1, :], g2[:, t - 1, :], ALU.min)
+
+        gs_b = gs4[:].rearrange("p (a t b) -> p a t b", a=1, b=1).to_broadcast([P, HALF // 4, PACK, 4])
+
+        def clamp_low(h, tag):
+            c = sb("c%d" % h, [P, PACK, HALF], F32, tag=tag)
+            nc.vector.tensor_tensor(c[:], m[:, :, h * HALF : (h + 1) * HALF], g3[h][:], ALU.max)
+            return c
+
+        def weigh(h, c):
+            zb = sb("zb%d" % h, [P, HALF * PACK], BF16)
+            nc.vector.tensor_tensor(
+                zb[:].rearrange("p (c i t) -> p c t i", i=4, t=PACK),
+                c[:].rearrange("p t (c i) -> p c t i", i=4), gs_b, ALU.mult)
+            return zb
+
+        def coded_layer(h, zb):
+            z_w = sb("z_w%d" % h, [P, HALF], U32)
+            z_s = sb("z_s%d" % h, [P, HALF], U8)
+            nc.vector.quantize_mx(out=z_w[:].bitcast(FP8X4), scales=z_s[:], in_=zb[:])
+            bank = psum.tile([P, 4, HALF], F32, name="h_bank%d" % h, tag="d_bank%d" % h)
+            for b in range(4):
+                cols = slice(b * P, (b + 1) * P)
+                nc.tensor.matmul_mx(
+                    out=bank[:, b, :], lhsT=dg_w[:, cols].bitcast(FP8X4), lhsT_scale=ds_placed[:, cols],
+                    rhs=z_w[:].bitcast(FP8X4), rhs_scale=z_s[:], start=True, stop=True)
+            return bank
+
+        c0 = clamp_low(0, "c0")
+        zb0 = weigh(0, c0)
+        c1 = clamp_low(1, "y_codes")
+        bank0 = coded_layer(0, zb0)
+        zb1 = weigh(1, c1)
+        bank1 = coded_layer(1, zb1)
+        h_banks = [bank0, bank1]
+
+        exc = sb("exc", [P, 4, S], F32)
+        for b in range(4):
+            nc.scalar.activation(ex[b][:, 0:HALF], h_banks[0][:, b, :], ACT.Exp, scale=0.03125)
+        nc.scalar.activation(exc[:, :, 0:HALF], h_banks[0][:], ACT.Exp, scale=0.03125)
+        g5 = sb("g5", [P, 4, S], F32)
+        nd = [sb("nd%d" % b, [P, 2, S], F32) for b in range(4)]
+        for b in range(5):
+            if b < 4:
+                nc.scalar.activation(ex[b][:, HALF:S], h_banks[1][:, b, :], ACT.Exp, scale=0.03125)
+                nc.vector.tensor_copy(exc[:, b, HALF:S], ex[b][:, HALF:S])
+            if b > 0:
+                nc.scalar.activation(g5[:, b - 1, :], ex[b - 1][:].indirect(n5_t[:]), ACT.Copy)
+                nc.vector.tensor_tensor(nd[b - 1][:, 0, :], ex[b - 1][:].indirect(n4_t[:]), exc[:, b - 1, :], ALU.add)
+                nc.vector.tensor_tensor(nd[b - 1][:, 1, :], ex[b - 1][:].indirect(n6_t[:]), g5[:, b - 1, :], ALU.add)
+        for b in range(4):
+            ln = sb("ln%d" % b, [P, 2, S], F32)
+            nc.scalar.activation(ln[:], nd[b][:], ACT.Ln)
+            res = sb("res%d" % b, [P, S], F32)
+            nc.vector.tensor_tensor(res[:], ln[:, 0, :], ln[:, 1, :], ALU.subtract)
+            nc.sync.dma_start(out[b * P : (b + 1) * P, :], res[:])

@@ -19,6 +19,7 @@ P = 128
 PACK = 4
 HALF = S // 2
 SPARE = 8
+SCALAR_SHARE = 44
 
 
 def tile_picked_twqclampbodds_none_p_kernel(
@@ -61,25 +62,22 @@ def tile_picked_twqclampbodds_none_p_kernel(
         two_t = load_list("two_t", two)
         offs_t = load_list("offs_t", offs)
 
-        def load_w(name, w):
-            rows = w.rearrange("(p j) c -> p j c", j=PACK)
-            parts = []
-            for u in range(2):
-                t = sb("%s_raw%d" % (name, u), [P, 2, H], F32)
-                nc.sync.dma_start(t[:], rows[:, 2 * u : 2 * u + 2, :])
-                parts.append(t)
-            return parts
 
-        w2_raw = load_w("w2", w2)
+        def load_w(name, w):
+            t = sb(name, [P, PACK, H], F32)
+            nc.sync.dma_start(t[:], w.rearrange("(p j) c -> p j c", j=PACK))
+            return t
+
+        w2_raw = load_w("w2_raw", w2)
         nc.sync.dma_start(xw_tab[:].bitcast(I32), x_words[0].rearrange("p n t -> p (n t)").bitcast(I32))
-        n2_t = load_list("n2_t", n2)
-        w1_raw = load_w("w1", w1)
-        n1_t = load_list("n1_t", n1)
-        n3_t = load_list("n3_t", n3)
         k1_t = load_list("k1_t", k1)
         ds_rows = d_scales[0].bitcast(I32)
         for r in range(2):
             nc.sync.dma_start(ds_tab[r:P:16, :].bitcast(I32), ds_rows[r:16:2, :])
+        n2_t = load_list("n2_t", n2)
+        w1_raw = load_w("w1_raw", w1)
+        n1_t = load_list("n1_t", n1)
+        n3_t = load_list("n3_t", n3)
         nc.sync.dma_start(dw_tab[:].bitcast(I32), d_words[0].rearrange("p n t -> p (n t)").bitcast(I32))
         gs4 = sb("gs4", [P, PACK], F32)
         nc.sync.dma_start(gs4[:], gs.rearrange("(p t) o -> p (t o)", t=PACK))
@@ -87,69 +85,69 @@ def tile_picked_twqclampbodds_none_p_kernel(
         n5_t = load_list("n5_t", n5)
         n6_t = load_list("n6_t", n6)
 
-        def cast_w(engine_copy, wb, raw, u):
-            dst = wb[:].rearrange("p (t m i j) -> p m t i j", t=PACK, i=2, j=PACK)[:, :, :, :, 2 * u : 2 * u + 2]
-            src = raw[:].rearrange("p j (m i t) -> p m t i j", i=2, t=PACK)
+        def cast_w(engine_copy, wb, raw, m0, m1):
+            dst = wb[:].rearrange("p (t m j) -> p m t j", t=PACK, j=PACK)[:, m0:m1]
+            src = raw[:].rearrange("p j (m t) -> p m t j", t=PACK)[:, m0:m1]
             engine_copy(dst, src)
 
-        def quantise_w(name, wb):
-            codes = sb(name + "_codes", [P, H], U32)
-            scales = sb(name + "_scales", [P, H], U8)
-            for v in range(2):
-                cols = slice(v * 2 * P, (v + 1) * 2 * P)
-                nc.vector.quantize_mx(
-                    out=codes[:, cols].bitcast(FP8X4), scales=scales[:, cols],
-                    in_=wb[:, v * 2 * P * PACK : (v + 1) * 2 * P * PACK])
-            return codes, scales
+        def quantise_w(codes, scales, wb, v):
+            cols = slice(v * 2 * P, (v + 1) * 2 * P)
+            nc.vector.quantize_mx(
+                out=codes[:, cols].bitcast(FP8X4), scales=scales[:, cols],
+                in_=wb[:, v * 2 * P * PACK : (v + 1) * 2 * P * PACK])
 
-        def project(name, codes, scales, x_w, x_s):
-            banks = []
+        def project(outs, codes, scales, x_w, x_s):
             for t in range(PACK):
-                bank = psum.tile([P, S], F32, name="%s_bank%d" % (name, t))
                 cols = slice(t * P, (t + 1) * P)
                 nc.tensor.matmul_mx(
-                    out=bank[:], lhsT=codes[:, cols].bitcast(FP8X4), lhsT_scale=scales[:, cols],
+                    out=outs[t], lhsT=codes[:, cols].bitcast(FP8X4), lhsT_scale=scales[:, cols],
                     rhs=x_w[:].bitcast(FP8X4), rhs_scale=x_s[:], start=True, stop=True)
-                banks.append(bank)
-            return banks
 
         x2_s = sb("x2_s", [P, S], U8)
         nc.vector.tensor_copy(x2_s[:], xs_tab[:].indirect(two_t[:]))
         x1_s = sb("x1_s", [P, S], U8)
         nc.vector.tensor_copy(x1_s[:], xs_tab[:].indirect(offs_t[:]))
         w2b = sb("w2b", [P, H * PACK], BF16)
-        cast_w(nc.scalar.copy, w2b, w2_raw[0], 0)
-        cast_w(nc.vector.tensor_copy, w2b, w2_raw[1], 1)
-        d_codes, d_sc = quantise_w("d", w2b)
+        cast_w(nc.scalar.copy, w2b, w2_raw, 0, SCALAR_SHARE)
+        cast_w(nc.vector.tensor_copy, w2b, w2_raw, SCALAR_SHARE, P)
+        d_codes = sb("d_codes", [P, H], U32)
+        d_sc = sb("d_scales", [P, H], U8)
+        quantise_w(d_codes, d_sc, w2b, 0)
         x2_w = sb("x2_w", [P, S], U32)
         nc.vector.tensor_copy(x2_w[:], xw_tab[:].indirect(two_t[:]))
-        d_banks = project("d", d_codes, d_sc, x2_w, x2_s)
+        quantise_w(d_codes, d_sc, w2b, 1)
+        x1_w = sb("x1_w", [P, S], U32, tag="w2_raw")
+        nc.vector.tensor_copy(x1_w[:], xw_tab[:].indirect(offs_t[:]))
+        d_ps = [psum.tile([P, S], F32, name="bank%d" % t)[:] for t in range(PACK)]
+        project(d_ps, d_codes, d_sc, x2_w, x2_s)
+
+        dg_s = sb("dg_s", [P, H], U8, tag="w2b")
+        nc.vector.tensor_copy(dg_s[:], ds_tab[:].indirect(k1_t[:]))
+        for i in range(4):
+            nc.sync.dma_start(ds_placed[i:P:32, :].bitcast(I32), dg_s[16 * (i // 2) + i % 2 : P : 32, :].bitcast(I32))
 
         g1 = sb("g1", [P, PACK, S], F32)
         g2 = sb("g2", [P, PACK, S], F32)
         for t in range(PACK + 1):
             if t < PACK:
-                nc.scalar.copy(d[t][:, :S], d_banks[t][:])
+                nc.scalar.copy(d[t][:, :S], d_ps[t])
             if t > 0:
                 nc.scalar.activation(g2[:, t - 1, :], d[t - 1][:].indirect(n2_t[:]), ACT.Copy)
 
-        x1_w = sb("x1_w", [P, S], U32)
-        nc.vector.tensor_copy(x1_w[:], xw_tab[:].indirect(offs_t[:]))
         w1b = sb("w1b", [P, H * PACK], BF16)
-        cast_w(nc.vector.tensor_copy, w1b, w1_raw[0], 0)
-        cast_w(nc.vector.tensor_copy, w1b, w1_raw[1], 1)
-        y_codes, y_sc = quantise_w("y", w1b)
-        y_banks = project("y", y_codes, y_sc, x1_w, x1_s)
-        for t in range(PACK + 1):
-            if t < PACK:
-                nc.scalar.copy(y[t][:, :S], y_banks[t][:])
-            if t > 0:
-                nc.scalar.activation(g1[:, t - 1, :], y[t - 1][:].indirect(n1_t[:]), ACT.Copy, scale=-0.5)
+        cast_w(nc.vector.tensor_copy, w1b, w1_raw, 0, P)
+        y_codes = sb("y_codes", [P, H], U32)
+        y_sc = sb("y_scales", [P, H], U8)
+        for v in range(2):
+            quantise_w(y_codes, y_sc, w1b, v)
+        y_pairs = [psum.tile([P, 2, S], F32, name="bank%d" % (4 + u)) for u in range(2)]
+        y_ps = [y_pairs[t // 2][:, t % 2, :] for t in range(PACK)]
+        project(y_ps, y_codes, y_sc, x1_w, x1_s)
+        for t in range(PACK):
+            (nc.scalar.copy if t < 2 else nc.vector.tensor_copy)(y[t][:, :S], y_ps[t])
+        for t in range(PACK):
+            nc.scalar.activation(g1[:, t, :], y[t][:].indirect(n1_t[:]), ACT.Copy, scale=-0.5)
 
-        dg_s = sb("dg_s", [P, H], U8, tag="w1b")
-        nc.vector.tensor_copy(dg_s[:], ds_tab[:].indirect(k1_t[:]))
-        for i in range(4):
-            nc.sync.dma_start(ds_placed[i:P:32, :].bitcast(I32), dg_s[16 * (i // 2) + i % 2 : P : 32, :].bitcast(I32))
         dg_w = sb("dg_w", [P, H], U32)
         nc.vector.tensor_copy(dg_w[:], dw_tab[:].indirect(k1_t[:]))
 
@@ -160,55 +158,58 @@ def tile_picked_twqclampbodds_none_p_kernel(
 
         a = sb("a", [P, PACK, S], F32, tag="dw_tab")
         m = sb("m", [P, PACK, S], F32)
-        for t in range(PACK + 1):
-            if t < PACK:
-                nc.vector.tensor_tensor(a[:, t, :], g1[:, t, :], y[t][:, :S], ALU.add)
-            if t > 0:
-                nc.vector.tensor_tensor(m[:, t - 1, :], a[:, t - 1, :], g2[:, t - 1, :], ALU.min)
+        for u in range(2):
+            pair = slice(2 * u, 2 * u + 2)
+            nc.vector.tensor_tensor(a[:, pair, :], g1[:, pair, :], y_pairs[u][:], ALU.add)
+        for u in range(2):
+            pair = slice(2 * u, 2 * u + 2)
+            nc.vector.tensor_tensor(m[:, pair, :], a[:, pair, :], g2[:, pair, :], ALU.min)
 
         gs_b = gs4[:].rearrange("p (a t b) -> p a t b", a=1, b=1).to_broadcast([P, HALF // 4, PACK, 4])
 
-        def clamp_low(h, tag):
-            c = sb("c%d" % h, [P, PACK, HALF], F32, tag=tag)
-            nc.vector.tensor_tensor(c[:], m[:, :, h * HALF : (h + 1) * HALF], g3[h][:], ALU.max)
-            return c
+        c = [sb("c0", [P, PACK, HALF], F32), sb("c1", [P, PACK, HALF], F32, tag="dw_tab")]
 
-        def weigh(h, c):
+        def clamp_low(h, u):
+            pair = slice(2 * u, 2 * u + 2)
+            nc.vector.tensor_tensor(c[h][:, pair, :], m[:, pair, h * HALF : (h + 1) * HALF], g3[h][:, pair, :], ALU.max)
+
+        def weigh(h, src):
             zb = sb("zb%d" % h, [P, HALF * PACK], BF16)
             nc.vector.tensor_tensor(
                 zb[:].rearrange("p (c i t) -> p c t i", i=4, t=PACK),
-                c[:].rearrange("p t (c i) -> p c t i", i=4), gs_b, ALU.mult)
+                src[:].rearrange("p t (c i) -> p c t i", i=4), gs_b, ALU.mult)
             return zb
 
         def coded_layer(h, zb):
             z_w = sb("z_w%d" % h, [P, HALF], U32)
             z_s = sb("z_s%d" % h, [P, HALF], U8)
             nc.vector.quantize_mx(out=z_w[:].bitcast(FP8X4), scales=z_s[:], in_=zb[:])
-            bank = psum.tile([P, 4, HALF], F32, name="h_bank%d" % h, tag="d_bank%d" % h)
+            outs = [psum.tile([P, HALF], F32, name="h%d_%d" % (h, b), tag="bank%d" % (4 * h + b))[:] for b in range(4)]
             for b in range(4):
                 cols = slice(b * P, (b + 1) * P)
                 nc.tensor.matmul_mx(
-                    out=bank[:, b, :], lhsT=dg_w[:, cols].bitcast(FP8X4), lhsT_scale=ds_placed[:, cols],
+                    out=outs[b], lhsT=dg_w[:, cols].bitcast(FP8X4), lhsT_scale=ds_placed[:, cols],
                     rhs=z_w[:].bitcast(FP8X4), rhs_scale=z_s[:], start=True, stop=True)
-            return bank
+            return outs
 
-        c0 = clamp_low(0, "c0")
-        zb0 = weigh(0, c0)
-        c1 = clamp_low(1, "y_codes")
-        bank0 = coded_layer(0, zb0)
-        zb1 = weigh(1, c1)
-        bank1 = coded_layer(1, zb1)
-        h_banks = [bank0, bank1]
+        clamp_low(0, 0)
+        clamp_low(0, 1)
+        clamp_low(1, 0)
+        zb0 = weigh(0, c[0])
+        clamp_low(1, 1)
+        outs0 = coded_layer(0, zb0)
+        zb1 = weigh(1, c[1])
+        outs1 = coded_layer(1, zb1)
 
         exc = sb("exc", [P, 4, S], F32)
         for b in range(4):
-            nc.scalar.activation(ex[b][:, 0:HALF], h_banks[0][:, b, :], ACT.Exp, scale=0.03125)
-        nc.scalar.activation(exc[:, :, 0:HALF], h_banks[0][:], ACT.Exp, scale=0.03125)
+            nc.scalar.activation(ex[b][:, 0:HALF], outs0[b], ACT.Exp, scale=0.03125)
+            nc.vector.tensor_copy(exc[:, b, 0:HALF], ex[b][:, 0:HALF])
         g5 = sb("g5", [P, 4, S], F32)
         nd = [sb("nd%d" % b, [P, 2, S], F32) for b in range(4)]
         for b in range(5):
             if b < 4:
-                nc.scalar.activation(ex[b][:, HALF:S], h_banks[1][:, b, :], ACT.Exp, scale=0.03125)
+                nc.scalar.activation(ex[b][:, HALF:S], outs1[b], ACT.Exp, scale=0.03125)
                 nc.vector.tensor_copy(exc[:, b, HALF:S], ex[b][:, HALF:S])
             if b > 0:
                 nc.scalar.activation(g5[:, b - 1, :], ex[b - 1][:].indirect(n5_t[:]), ACT.Copy)

@@ -19,6 +19,7 @@ P = 128
 PACK = 4
 HALF = S // 2
 SPARE = 8
+SPARE_VECTOR = 96
 SCALAR_SHARE = 44
 
 
@@ -48,7 +49,7 @@ def tile_picked_twqclampbodds_none_p_kernel(
         dw_tab = sb("dw_tab", [P, G], U32)
         ex = [sb("ex%d" % b, [P, S + SPARE], F32) for b in range(4)]
         y = [sb("y%d" % t, [P, S + SPARE], F32) for t in range(PACK)]
-        d = [sb("d%d" % t, [P, S + SPARE], F32) for t in range(PACK)]
+        d = [sb("d%d" % t, [P, S + (SPARE if t < PACK - 1 else SPARE_VECTOR)], F32) for t in range(PACK)]
 
         nc.gpsimd.memset(ds_tab[:].bitcast(I32), 0)
         nc.gpsimd.memset(ds_placed[:].bitcast(I32), 0)
@@ -75,7 +76,10 @@ def tile_picked_twqclampbodds_none_p_kernel(
         for r in range(2):
             nc.sync.dma_start(ds_tab[r:P:16, :].bitcast(I32), ds_rows[r:16:2, :])
         n2_t = load_list("n2_t", n2)
-        w1_raw = load_w("w1_raw", w1)
+        w1_rows = w1.rearrange("(p j) c -> p j c", j=PACK)
+        w1_raw = [sb("w1_raw%d" % u, [P, 2, H], F32) for u in range(2)]
+        for u in range(2):
+            nc.sync.dma_start(w1_raw[u][:], w1_rows[:, 2 * u : 2 * u + 2, :])
         n1_t = load_list("n1_t", n1)
         n3_t = load_list("n3_t", n3)
         nc.sync.dma_start(dw_tab[:].bitcast(I32), d_words[0].rearrange("p n t -> p (n t)").bitcast(I32))
@@ -121,30 +125,32 @@ def tile_picked_twqclampbodds_none_p_kernel(
         d_ps = [psum.tile([P, S], F32, name="bank%d" % t)[:] for t in range(PACK)]
         project(d_ps, d_codes, d_sc, x2_w, x2_s)
 
-        dg_s = sb("dg_s", [P, H], U8, tag="w2b")
-        nc.vector.tensor_copy(dg_s[:], ds_tab[:].indirect(k1_t[:]))
-        for i in range(4):
-            nc.sync.dma_start(ds_placed[i:P:32, :].bitcast(I32), dg_s[16 * (i // 2) + i % 2 : P : 32, :].bitcast(I32))
-
         g1 = sb("g1", [P, PACK, S], F32)
-        g2 = sb("g2", [P, PACK, S], F32)
-        for t in range(PACK + 1):
-            if t < PACK:
-                nc.scalar.copy(d[t][:, :S], d_ps[t])
+        g2 = [sb("g2_%d" % t, [P, S], F32) for t in range(PACK - 1)]
+        for t in range(PACK):
+            nc.scalar.copy(d[t][:, :S], d_ps[t])
             if t > 0:
-                nc.scalar.activation(g2[:, t - 1, :], d[t - 1][:].indirect(n2_t[:]), ACT.Copy)
+                nc.scalar.activation(g2[t - 1][:], d[t - 1][:].indirect(n2_t[:]), ACT.Copy)
 
         w1b = sb("w1b", [P, H * PACK], BF16)
-        cast_w(nc.vector.tensor_copy, w1b, w1_raw, 0, P)
+        for u in range(2):
+            dst = w1b[:].rearrange("p (t m i j) -> p m t i j", t=PACK, i=2, j=PACK)[:, :, :, :, 2 * u : 2 * u + 2]
+            nc.vector.tensor_copy(dst, w1_raw[u][:].rearrange("p j (m i t) -> p m t i j", i=2, t=PACK))
         y_codes = sb("y_codes", [P, H], U32)
         y_sc = sb("y_scales", [P, H], U8)
         for v in range(2):
             quantise_w(y_codes, y_sc, w1b, v)
-        y_pairs = [psum.tile([P, 2, S], F32, name="bank%d" % (4 + u)) for u in range(2)]
-        y_ps = [y_pairs[t // 2][:, t % 2, :] for t in range(PACK)]
+        y_ps = [psum.tile([P, S], F32, name="bank%d" % (4 + t))[:] for t in range(PACK)]
         project(y_ps, y_codes, y_sc, x1_w, x1_s)
+        dg_s = sb("dg_s", [P, H], U8, tag="w1_raw1")
+        nc.vector.tensor_copy(dg_s[:], ds_tab[:].indirect(k1_t[:]))
+        for i in range(4):
+            nc.sync.dma_start(ds_placed[i:P:32, :].bitcast(I32), dg_s[16 * (i // 2) + i % 2 : P : 32, :].bitcast(I32))
+
+        g2.append(sb("g2_3", [P, S], F32, tag="w1b"))
+        nc.vector.tensor_copy(g2[3][:], d[3][:].indirect(n2_t[:]))
         for t in range(PACK):
-            (nc.scalar.copy if t < 2 else nc.vector.tensor_copy)(y[t][:, :S], y_ps[t])
+            (nc.scalar.copy if t < 3 else nc.vector.tensor_copy)(y[t][:, :S], y_ps[t])
         for t in range(PACK):
             nc.scalar.activation(g1[:, t, :], y[t][:].indirect(n1_t[:]), ACT.Copy, scale=-0.5)
 
@@ -158,12 +164,11 @@ def tile_picked_twqclampbodds_none_p_kernel(
 
         a = sb("a", [P, PACK, S], F32, tag="dw_tab")
         m = sb("m", [P, PACK, S], F32)
-        for u in range(2):
-            pair = slice(2 * u, 2 * u + 2)
-            nc.vector.tensor_tensor(a[:, pair, :], g1[:, pair, :], y_pairs[u][:], ALU.add)
-        for u in range(2):
-            pair = slice(2 * u, 2 * u + 2)
-            nc.vector.tensor_tensor(m[:, pair, :], a[:, pair, :], g2[:, pair, :], ALU.min)
+        for t in range(PACK + 1):
+            if t < PACK:
+                nc.vector.tensor_tensor(a[:, t, :], g1[:, t, :], y[t][:, :S], ALU.add)
+            if t > 0:
+                nc.vector.tensor_tensor(m[:, t - 1, :], a[:, t - 1, :], g2[t - 1][:], ALU.min)
 
         gs_b = gs4[:].rearrange("p (a t b) -> p a t b", a=1, b=1).to_broadcast([P, HALF // 4, PACK, 4])
 
@@ -210,14 +215,23 @@ def tile_picked_twqclampbodds_none_p_kernel(
         for b in range(5):
             if b < 4:
                 nc.scalar.activation(ex[b][:, HALF:S], outs1[b], ACT.Exp, scale=0.03125)
+                if b == 0:
+                    nc.vector.tensor_tensor(nd[0][:, 0, :HALF], ex[0][:].indirect(half_of(n4_t, 0)), exc[:, 0, :HALF], ALU.add)
                 nc.vector.tensor_copy(exc[:, b, HALF:S], ex[b][:, HALF:S])
             if b > 0:
                 nc.scalar.activation(g5[:, b - 1, :], ex[b - 1][:].indirect(n5_t[:]), ACT.Copy)
-                nc.vector.tensor_tensor(nd[b - 1][:, 0, :], ex[b - 1][:].indirect(n4_t[:]), exc[:, b - 1, :], ALU.add)
+                if b > 1:
+                    nc.vector.tensor_tensor(nd[b - 1][:, 0, :], ex[b - 1][:].indirect(n4_t[:]), exc[:, b - 1, :], ALU.add)
+                else:
+                    nc.vector.tensor_tensor(nd[0][:, 0, HALF:], ex[0][:].indirect(half_of(n4_t, 1)), exc[:, 0, HALF:], ALU.add)
                 nc.vector.tensor_tensor(nd[b - 1][:, 1, :], ex[b - 1][:].indirect(n6_t[:]), g5[:, b - 1, :], ALU.add)
         for b in range(4):
             ln = sb("ln%d" % b, [P, 2, S], F32)
-            nc.scalar.activation(ln[:], nd[b][:], ACT.Ln)
+            if b < 3:
+                nc.scalar.activation(ln[:], nd[b][:], ACT.Ln)
+            else:
+                nc.scalar.activation(ln[:, 0, :], nd[b][:, 0, :], ACT.Ln)
+                nc.scalar.activation(ln[:, 1, :], nd[b][:, 1, :], ACT.Ln)
             res = sb("res%d" % b, [P, S], F32)
             nc.vector.tensor_tensor(res[:], ln[:, 0, :], ln[:, 1, :], ALU.subtract)
             nc.sync.dma_start(out[b * P : (b + 1) * P, :], res[:])

@@ -17,10 +17,12 @@ ACT = mybir.ActivationFunctionType
 
 P = 128
 PACK = 4
+BLOCKS = H // P
 HALF = S // 2
 SPARE = 8
 SPARE_VECTOR = 96
 SCALAR_SHARE = 44
+EXP_SCALE = 0.5 * 0.0625
 
 
 def tile_picked_twqclampbodds_none_p_kernel(
@@ -35,26 +37,29 @@ def tile_picked_twqclampbodds_none_p_kernel(
             return keep.tile(shape, dtype, name=name, align_bytes=64, tag=tag or name)
 
         def load_list(name, src):
-            t = sb(name, list(src.shape), U16)
-            nc.sync.dma_start(t[:], src)
-            return t
+            lst = sb(name, list(src.shape), U16)
+            nc.sync.dma_start(lst[:], src)
+            return lst
 
         def half_of(lst, h):
             return lst[:, h * HALF // 16 : (h + 1) * HALF // 16]
+
+        def places(h):
+            return slice(h * HALF, (h + 1) * HALF)
 
         xs_tab = sb("xs_tab", [P, T], U8)
         ds_tab = sb("ds_tab", [P, G], U8)
         ds_placed = sb("ds_placed", [P, H], U8)
         xw_tab = sb("xw_tab", [P, T], U32)
         dw_tab = sb("dw_tab", [P, G], U32)
-        ex = [sb("ex%d" % b, [P, S + SPARE], F32) for b in range(4)]
+        ex = [sb("ex%d" % b, [P, S + SPARE], F32) for b in range(BLOCKS)]
         y = [sb("y%d" % t, [P, S + SPARE], F32) for t in range(PACK)]
         d = [sb("d%d" % t, [P, S + (SPARE if t < PACK - 1 else SPARE_VECTOR)], F32) for t in range(PACK)]
 
         nc.gpsimd.memset(ds_tab[:].bitcast(I32), 0)
         nc.gpsimd.memset(ds_placed[:].bitcast(I32), 0)
-        for win in d + y + ex:
-            nc.gpsimd.memset(win[:, S:], 0.0)
+        for window in d + y + ex:
+            nc.gpsimd.memset(window[:, S:], 0.0)
 
         xs_rows = x_scales[0].bitcast(I32)
         for q in range(4):
@@ -62,14 +67,8 @@ def tile_picked_twqclampbodds_none_p_kernel(
             nc.sync.dma_start(xs_tab[32 * q : 32 * q + 32, :].bitcast(I32), rows)
         two_t = load_list("two_t", two)
         offs_t = load_list("offs_t", offs)
-
-
-        def load_w(name, w):
-            t = sb(name, [P, PACK, H], F32)
-            nc.sync.dma_start(t[:], w.rearrange("(p j) c -> p j c", j=PACK))
-            return t
-
-        w2_raw = load_w("w2_raw", w2)
+        w2_raw = sb("w2_raw", [P, PACK, H], F32)
+        nc.sync.dma_start(w2_raw[:], w2.rearrange("(p j) c -> p j c", j=PACK))
         nc.sync.dma_start(xw_tab[:].bitcast(I32), x_words[0].rearrange("p n t -> p (n t)").bitcast(I32))
         k1_t = load_list("k1_t", k1)
         ds_rows = d_scales[0].bitcast(I32)
@@ -89,41 +88,38 @@ def tile_picked_twqclampbodds_none_p_kernel(
         n5_t = load_list("n5_t", n5)
         n6_t = load_list("n6_t", n6)
 
-        def cast_w(engine_copy, wb, raw, m0, m1):
-            dst = wb[:].rearrange("p (t m j) -> p m t j", t=PACK, j=PACK)[:, m0:m1]
-            src = raw[:].rearrange("p j (m t) -> p m t j", t=PACK)[:, m0:m1]
-            engine_copy(dst, src)
-
         def quantise_w(codes, scales, wb, v):
             cols = slice(v * 2 * P, (v + 1) * 2 * P)
             nc.vector.quantize_mx(
                 out=codes[:, cols].bitcast(FP8X4), scales=scales[:, cols],
                 in_=wb[:, v * 2 * P * PACK : (v + 1) * 2 * P * PACK])
 
-        def project(outs, codes, scales, x_w, x_s):
-            for t in range(PACK):
-                cols = slice(t * P, (t + 1) * P)
+        def product(outs, lhs_w, lhs_s, rhs_w, rhs_s):
+            for i in range(len(outs)):
+                cols = slice(i * P, (i + 1) * P)
                 nc.tensor.matmul_mx(
-                    out=outs[t], lhsT=codes[:, cols].bitcast(FP8X4), lhsT_scale=scales[:, cols],
-                    rhs=x_w[:].bitcast(FP8X4), rhs_scale=x_s[:], start=True, stop=True)
+                    out=outs[i], lhsT=lhs_w[:, cols].bitcast(FP8X4), lhsT_scale=lhs_s[:, cols],
+                    rhs=rhs_w[:].bitcast(FP8X4), rhs_scale=rhs_s[:], start=True, stop=True)
 
         x2_s = sb("x2_s", [P, S], U8)
         nc.vector.tensor_copy(x2_s[:], xs_tab[:].indirect(two_t[:]))
         x1_s = sb("x1_s", [P, S], U8)
         nc.vector.tensor_copy(x1_s[:], xs_tab[:].indirect(offs_t[:]))
         w2b = sb("w2b", [P, H * PACK], BF16)
-        cast_w(nc.scalar.copy, w2b, w2_raw, 0, SCALAR_SHARE)
-        cast_w(nc.vector.tensor_copy, w2b, w2_raw, SCALAR_SHARE, P)
-        d_codes = sb("d_codes", [P, H], U32)
-        d_sc = sb("d_scales", [P, H], U8)
-        quantise_w(d_codes, d_sc, w2b, 0)
+        w2_dst = w2b[:].rearrange("p (t m j) -> p m t j", t=PACK, j=PACK)
+        w2_src = w2_raw[:].rearrange("p j (m t) -> p m t j", t=PACK)
+        nc.scalar.copy(w2_dst[:, 0:SCALAR_SHARE], w2_src[:, 0:SCALAR_SHARE])
+        nc.vector.tensor_copy(w2_dst[:, SCALAR_SHARE:P], w2_src[:, SCALAR_SHARE:P])
+        w2_codes = sb("d_codes", [P, H], U32)
+        w2_scales = sb("d_scales", [P, H], U8)
+        quantise_w(w2_codes, w2_scales, w2b, 0)
         x2_w = sb("x2_w", [P, S], U32)
         nc.vector.tensor_copy(x2_w[:], xw_tab[:].indirect(two_t[:]))
-        quantise_w(d_codes, d_sc, w2b, 1)
+        quantise_w(w2_codes, w2_scales, w2b, 1)
         x1_w = sb("x1_w", [P, S], U32, tag="w2_raw")
         nc.vector.tensor_copy(x1_w[:], xw_tab[:].indirect(offs_t[:]))
         d_ps = [psum.tile([P, S], F32, name="bank%d" % t)[:] for t in range(PACK)]
-        project(d_ps, d_codes, d_sc, x2_w, x2_s)
+        product(d_ps, w2_codes, w2_scales, x2_w, x2_s)
 
         g1 = sb("g1", [P, PACK, S], F32)
         g2 = [sb("g2_%d" % t, [P, S], F32) for t in range(PACK - 1)]
@@ -134,25 +130,28 @@ def tile_picked_twqclampbodds_none_p_kernel(
 
         w1b = sb("w1b", [P, H * PACK], BF16)
         for u in range(2):
-            dst = w1b[:].rearrange("p (t m i j) -> p m t i j", t=PACK, i=2, j=PACK)[:, :, :, :, 2 * u : 2 * u + 2]
-            nc.vector.tensor_copy(dst, w1_raw[u][:].rearrange("p j (m i t) -> p m t i j", i=2, t=PACK))
-        y_codes = sb("y_codes", [P, H], U32)
-        y_sc = sb("y_scales", [P, H], U8)
+            w1_dst = w1b[:].rearrange("p (t m i j) -> p m t i j", t=PACK, i=2, j=PACK)[:, :, :, :, 2 * u : 2 * u + 2]
+            nc.vector.tensor_copy(w1_dst, w1_raw[u][:].rearrange("p j (m i t) -> p m t i j", i=2, t=PACK))
+        w1_codes = sb("y_codes", [P, H], U32)
+        w1_scales = sb("y_scales", [P, H], U8)
         for v in range(2):
-            quantise_w(y_codes, y_sc, w1b, v)
-        y_ps = [psum.tile([P, S], F32, name="bank%d" % (4 + t))[:] for t in range(PACK)]
-        project(y_ps, y_codes, y_sc, x1_w, x1_s)
+            quantise_w(w1_codes, w1_scales, w1b, v)
+        y_ps = [psum.tile([P, S], F32, name="bank%d" % (PACK + t))[:] for t in range(PACK)]
+        product(y_ps, w1_codes, w1_scales, x1_w, x1_s)
+
         dg_s = sb("dg_s", [P, H], U8, tag="w1_raw1")
         nc.vector.tensor_copy(dg_s[:], ds_tab[:].indirect(k1_t[:]))
-        for i in range(4):
-            nc.sync.dma_start(ds_placed[i:P:32, :].bitcast(I32), dg_s[16 * (i // 2) + i % 2 : P : 32, :].bitcast(I32))
+        for r in range(4):
+            nc.sync.dma_start(ds_placed[r:P:32, :].bitcast(I32), dg_s[16 * (r // 2) + r % 2 : P : 32, :].bitcast(I32))
 
         g2.append(sb("g2_3", [P, S], F32, tag="w1b"))
-        nc.vector.tensor_copy(g2[3][:], d[3][:].indirect(n2_t[:]))
-        for t in range(PACK):
-            (nc.scalar.copy if t < 3 else nc.vector.tensor_copy)(y[t][:, :S], y_ps[t])
-        for t in range(PACK):
-            nc.scalar.activation(g1[:, t, :], y[t][:].indirect(n1_t[:]), ACT.Copy, scale=-0.5)
+        nc.vector.tensor_copy(g2[PACK - 1][:], d[PACK - 1][:].indirect(n2_t[:]))
+
+        for t in range(PACK + 1):
+            if t < PACK:
+                nc.scalar.copy(y[t][:, :S], y_ps[t])
+            if t > 0:
+                nc.scalar.activation(g1[:, t - 1, :], y[t - 1][:].indirect(n1_t[:]), ACT.Copy, scale=-0.5)
 
         dg_w = sb("dg_w", [P, H], U32)
         nc.vector.tensor_copy(dg_w[:], dw_tab[:].indirect(k1_t[:]))
@@ -162,76 +161,77 @@ def tile_picked_twqclampbodds_none_p_kernel(
             for t in range(PACK):
                 nc.scalar.activation(g3[h][:, t, :], d[t][:].indirect(half_of(n3_t, h)), ACT.Copy)
 
-        a = sb("a", [P, PACK, S], F32, tag="dw_tab")
-        m = sb("m", [P, PACK, S], F32)
+        diff = sb("a", [P, PACK, S], F32, tag="dw_tab")
+        upper = sb("m", [P, PACK, S], F32)
         for t in range(PACK + 1):
             if t < PACK:
-                nc.vector.tensor_tensor(a[:, t, :], g1[:, t, :], y[t][:, :S], ALU.add)
+                nc.vector.tensor_tensor(diff[:, t, :], g1[:, t, :], y[t][:, :S], ALU.add)
             if t > 0:
-                nc.vector.tensor_tensor(m[:, t - 1, :], a[:, t - 1, :], g2[t - 1][:], ALU.min)
+                nc.vector.tensor_tensor(upper[:, t - 1, :], diff[:, t - 1, :], g2[t - 1][:], ALU.min)
 
         gs_b = gs4[:].rearrange("p (a t b) -> p a t b", a=1, b=1).to_broadcast([P, HALF // 4, PACK, 4])
+        clamped = [sb("c0", [P, PACK, HALF], F32), sb("c1", [P, PACK, HALF], F32, tag="dw_tab")]
 
-        c = [sb("c0", [P, PACK, HALF], F32), sb("c1", [P, PACK, HALF], F32, tag="dw_tab")]
-
-        def clamp_low(h, u):
+        def clamp(h, u):
             pair = slice(2 * u, 2 * u + 2)
-            nc.vector.tensor_tensor(c[h][:, pair, :], m[:, pair, h * HALF : (h + 1) * HALF], g3[h][:, pair, :], ALU.max)
+            nc.vector.tensor_tensor(clamped[h][:, pair, :], upper[:, pair, places(h)], g3[h][:, pair, :], ALU.max)
 
-        def weigh(h, src):
+        def weigh(h):
             zb = sb("zb%d" % h, [P, HALF * PACK], BF16)
             nc.vector.tensor_tensor(
                 zb[:].rearrange("p (c i t) -> p c t i", i=4, t=PACK),
-                src[:].rearrange("p t (c i) -> p c t i", i=4), gs_b, ALU.mult)
+                clamped[h][:].rearrange("p t (c i) -> p c t i", i=4), gs_b, ALU.mult)
             return zb
 
         def coded_layer(h, zb):
             z_w = sb("z_w%d" % h, [P, HALF], U32)
             z_s = sb("z_s%d" % h, [P, HALF], U8)
             nc.vector.quantize_mx(out=z_w[:].bitcast(FP8X4), scales=z_s[:], in_=zb[:])
-            outs = [psum.tile([P, HALF], F32, name="h%d_%d" % (h, b), tag="bank%d" % (4 * h + b))[:] for b in range(4)]
-            for b in range(4):
-                cols = slice(b * P, (b + 1) * P)
-                nc.tensor.matmul_mx(
-                    out=outs[b], lhsT=dg_w[:, cols].bitcast(FP8X4), lhsT_scale=ds_placed[:, cols],
-                    rhs=z_w[:].bitcast(FP8X4), rhs_scale=z_s[:], start=True, stop=True)
+            outs = [
+                psum.tile([P, HALF], F32, name="h%d_%d" % (h, b), tag="bank%d" % (BLOCKS * h + b))[:]
+                for b in range(BLOCKS)
+            ]
+            product(outs, dg_w, ds_placed, z_w, z_s)
             return outs
 
-        clamp_low(0, 0)
-        clamp_low(0, 1)
-        clamp_low(1, 0)
-        zb0 = weigh(0, c[0])
-        clamp_low(1, 1)
-        outs0 = coded_layer(0, zb0)
-        zb1 = weigh(1, c[1])
-        outs1 = coded_layer(1, zb1)
+        clamp(0, 0)
+        clamp(0, 1)
+        clamp(1, 0)
+        zb0 = weigh(0)
+        clamp(1, 1)
+        h_first = coded_layer(0, zb0)
+        zb1 = weigh(1)
+        h_second = coded_layer(1, zb1)
 
-        exc = sb("exc", [P, 4, S], F32)
-        for b in range(4):
-            nc.scalar.activation(ex[b][:, 0:HALF], outs0[b], ACT.Exp, scale=0.03125)
-            nc.vector.tensor_copy(exc[:, b, 0:HALF], ex[b][:, 0:HALF])
-        g5 = sb("g5", [P, 4, S], F32)
-        nd = [sb("nd%d" % b, [P, 2, S], F32) for b in range(4)]
-        for b in range(5):
-            if b < 4:
-                nc.scalar.activation(ex[b][:, HALF:S], outs1[b], ACT.Exp, scale=0.03125)
+        ex_copy = sb("exc", [P, BLOCKS, S], F32)
+        for b in range(BLOCKS):
+            nc.scalar.activation(ex[b][:, places(0)], h_first[b], ACT.Exp, scale=EXP_SCALE)
+            nc.vector.tensor_copy(ex_copy[:, b, places(0)], ex[b][:, places(0)])
+        g5 = sb("g5", [P, BLOCKS, S], F32)
+        sums = [sb("nd%d" % b, [P, 2, S], F32) for b in range(BLOCKS)]
+
+        def numerator(b, cols, offsets):
+            nc.vector.tensor_tensor(sums[b][:, 0, cols], ex[b][:].indirect(offsets), ex_copy[:, b, cols], ALU.add)
+
+        for b in range(BLOCKS + 1):
+            if b < BLOCKS:
+                nc.scalar.activation(ex[b][:, places(1)], h_second[b], ACT.Exp, scale=EXP_SCALE)
                 if b == 0:
-                    nc.vector.tensor_tensor(nd[0][:, 0, :HALF], ex[0][:].indirect(half_of(n4_t, 0)), exc[:, 0, :HALF], ALU.add)
-                nc.vector.tensor_copy(exc[:, b, HALF:S], ex[b][:, HALF:S])
+                    numerator(0, places(0), half_of(n4_t, 0))
+                nc.vector.tensor_copy(ex_copy[:, b, places(1)], ex[b][:, places(1)])
             if b > 0:
-                nc.scalar.activation(g5[:, b - 1, :], ex[b - 1][:].indirect(n5_t[:]), ACT.Copy)
-                if b > 1:
-                    nc.vector.tensor_tensor(nd[b - 1][:, 0, :], ex[b - 1][:].indirect(n4_t[:]), exc[:, b - 1, :], ALU.add)
+                prev = b - 1
+                nc.scalar.activation(g5[:, prev, :], ex[prev][:].indirect(n5_t[:]), ACT.Copy)
+                if prev == 0:
+                    numerator(0, places(1), half_of(n4_t, 1))
                 else:
-                    nc.vector.tensor_tensor(nd[0][:, 0, HALF:], ex[0][:].indirect(half_of(n4_t, 1)), exc[:, 0, HALF:], ALU.add)
-                nc.vector.tensor_tensor(nd[b - 1][:, 1, :], ex[b - 1][:].indirect(n6_t[:]), g5[:, b - 1, :], ALU.add)
-        for b in range(4):
-            ln = sb("ln%d" % b, [P, 2, S], F32)
-            if b < 3:
-                nc.scalar.activation(ln[:], nd[b][:], ACT.Ln)
-            else:
-                nc.scalar.activation(ln[:, 0, :], nd[b][:, 0, :], ACT.Ln)
-                nc.scalar.activation(ln[:, 1, :], nd[b][:, 1, :], ACT.Ln)
+                    numerator(prev, slice(0, S), n4_t[:])
+                nc.vector.tensor_tensor(sums[prev][:, 1, :], ex[prev][:].indirect(n6_t[:]), g5[:, prev, :], ALU.add)
+
+        for b in range(BLOCKS):
+            logs = sb("ln%d" % b, [P, 2, S], F32)
             res = sb("res%d" % b, [P, S], F32)
-            nc.vector.tensor_tensor(res[:], ln[:, 0, :], ln[:, 1, :], ALU.subtract)
-            nc.sync.dma_start(out[b * P : (b + 1) * P, :], res[:])
+            for cols in [slice(0, S)] if b < BLOCKS - 1 else [places(0), places(1)]:
+                nc.scalar.activation(logs[:, :, cols], sums[b][:, :, cols], ACT.Ln)
+                nc.vector.tensor_tensor(res[:, cols], logs[:, 0, cols], logs[:, 1, cols], ALU.subtract)
+                nc.sync.dma_start(out[b * P : (b + 1) * P, cols], res[:, cols])

from contextlib import ExitStack

import concourse.mybir as mybir

K, T, S, H, G = 512, 1024, 256, 512, 2048
FLOPS = 3 * 2 * K * H * S

F32 = mybir.dt.float32
BF16 = mybir.dt.bfloat16
I32 = mybir.dt.int32
U32 = mybir.dt.uint32
U16 = mybir.dt.uint16
U8 = mybir.dt.uint8
FP8X4 = mybir.dt.float8_e4m3fn_x4
ALU = mybir.AluOpType
ACT = mybir.ActivationFunctionType

P = 128
PACK = 4
BLOCKS = H // P
HALF = S // 2
SPARE = 8
SPARE_VECTOR = 96
SCALAR_SHARE = 44
EXP_SCALE = 0.5 * 0.0625


def tile_picked_twqclampbodds_none_p_kernel(
    tc, x_words, x_scales, w1, w2, gs, d_words, d_scales, offs, two, n1, n2, n3, k1, n4, n5, n6, out
):
    nc = tc.nc
    with ExitStack() as ctx:
        keep = ctx.enter_context(tc.tile_pool(name="keep", bufs=1))
        psum = ctx.enter_context(tc.psum_pool(name="psum", bufs=1))

        def sb(name, shape, dtype, tag=""):
            return keep.tile(shape, dtype, name=name, align_bytes=64, tag=tag or name)

        def load_list(name, src):
            lst = sb(name, list(src.shape), U16)
            nc.sync.dma_start(lst[:], src)
            return lst

        def half_of(lst, h):
            return lst[:, h * HALF // 16 : (h + 1) * HALF // 16]

        def places(h):
            return slice(h * HALF, (h + 1) * HALF)

        xs_tab = sb("xs_tab", [P, T], U8)
        ds_tab = sb("ds_tab", [P, G], U8)
        ds_placed = sb("ds_placed", [P, H], U8)
        xw_tab = sb("xw_tab", [P, T], U32)
        dw_tab = sb("dw_tab", [P, G], U32)
        ex = [sb("ex%d" % b, [P, S + SPARE], F32) for b in range(BLOCKS)]
        y = [sb("y%d" % t, [P, S + SPARE], F32) for t in range(PACK)]
        d = [sb("d%d" % t, [P, S + (SPARE if t < PACK - 1 else SPARE_VECTOR)], F32) for t in range(PACK)]

        nc.gpsimd.memset(ds_tab[:].bitcast(I32), 0)
        nc.gpsimd.memset(ds_placed[:].bitcast(I32), 0)
        for window in d + y + ex:
            nc.gpsimd.memset(window[:, S:], 0.0)

        xs_rows = x_scales[0].bitcast(I32)
        for q in range(4):
            rows = xs_rows[4 * q : 4 * q + 4, :].rearrange("(a r) c -> a r c", a=1).to_broadcast([8, 4, T // 4])
            nc.sync.dma_start(xs_tab[32 * q : 32 * q + 32, :].bitcast(I32), rows)
        two_t = load_list("two_t", two)
        offs_t = load_list("offs_t", offs)
        w2_raw = sb("w2_raw", [P, PACK, H], F32)
        nc.sync.dma_start(w2_raw[:], w2.rearrange("(p j) c -> p j c", j=PACK))
        nc.sync.dma_start(xw_tab[:].bitcast(I32), x_words[0].rearrange("p n t -> p (n t)").bitcast(I32))
        k1_t = load_list("k1_t", k1)
        ds_rows = d_scales[0].bitcast(I32)
        for r in range(2):
            nc.sync.dma_start(ds_tab[r:P:16, :].bitcast(I32), ds_rows[r:16:2, :])
        n2_t = load_list("n2_t", n2)
        w1_rows = w1.rearrange("(p j) c -> p j c", j=PACK)
        w1_raw = [sb("w1_raw%d" % u, [P, 2, H], F32) for u in range(2)]
        for u in range(2):
            nc.sync.dma_start(w1_raw[u][:], w1_rows[:, 2 * u : 2 * u + 2, :])
        n1_t = load_list("n1_t", n1)
        n3_t = load_list("n3_t", n3)
        nc.sync.dma_start(dw_tab[:].bitcast(I32), d_words[0].rearrange("p n t -> p (n t)").bitcast(I32))
        gs4 = sb("gs4", [P, PACK], F32)
        nc.sync.dma_start(gs4[:], gs.rearrange("(p t) o -> p (t o)", t=PACK))
        n4_t = load_list("n4_t", n4)
        n5_t = load_list("n5_t", n5)
        n6_t = load_list("n6_t", n6)

        def quantise_w(codes, scales, wb, v):
            cols = slice(v * 2 * P, (v + 1) * 2 * P)
            nc.vector.quantize_mx(
                out=codes[:, cols].bitcast(FP8X4), scales=scales[:, cols],
                in_=wb[:, v * 2 * P * PACK : (v + 1) * 2 * P * PACK])

        def product(outs, lhs_w, lhs_s, rhs_w, rhs_s):
            for i in range(len(outs)):
                cols = slice(i * P, (i + 1) * P)
                nc.tensor.matmul_mx(
                    out=outs[i], lhsT=lhs_w[:, cols].bitcast(FP8X4), lhsT_scale=lhs_s[:, cols],
                    rhs=rhs_w[:].bitcast(FP8X4), rhs_scale=rhs_s[:], start=True, stop=True)

        x2_s = sb("x2_s", [P, S], U8)
        nc.vector.tensor_copy(x2_s[:], xs_tab[:].indirect(two_t[:]))
        x1_s = sb("x1_s", [P, S], U8)
        nc.vector.tensor_copy(x1_s[:], xs_tab[:].indirect(offs_t[:]))
        w2b = sb("w2b", [P, H * PACK], BF16)
        w2_dst = w2b[:].rearrange("p (t m j) -> p m t j", t=PACK, j=PACK)
        w2_src = w2_raw[:].rearrange("p j (m t) -> p m t j", t=PACK)
        nc.scalar.copy(w2_dst[:, 0:SCALAR_SHARE], w2_src[:, 0:SCALAR_SHARE])
        nc.vector.tensor_copy(w2_dst[:, SCALAR_SHARE:P], w2_src[:, SCALAR_SHARE:P])
        w2_codes = sb("d_codes", [P, H], U32)
        w2_scales = sb("d_scales", [P, H], U8)
        quantise_w(w2_codes, w2_scales, w2b, 0)
        x2_w = sb("x2_w", [P, S], U32)
        nc.vector.tensor_copy(x2_w[:], xw_tab[:].indirect(two_t[:]))
        quantise_w(w2_codes, w2_scales, w2b, 1)
        x1_w = sb("x1_w", [P, S], U32, tag="w2_raw")
        nc.vector.tensor_copy(x1_w[:], xw_tab[:].indirect(offs_t[:]))
        d_ps = [psum.tile([P, S], F32, name="bank%d" % t)[:] for t in range(PACK)]
        product(d_ps, w2_codes, w2_scales, x2_w, x2_s)

        g1 = sb("g1", [P, PACK, S], F32)
        g2 = [sb("g2_%d" % t, [P, S], F32) for t in range(PACK - 1)]
        for t in range(PACK):
            nc.scalar.copy(d[t][:, :S], d_ps[t])
            if t > 0:
                nc.scalar.activation(g2[t - 1][:], d[t - 1][:].indirect(n2_t[:]), ACT.Copy)

        w1b = sb("w1b", [P, H * PACK], BF16)
        for u in range(2):
            w1_dst = w1b[:].rearrange("p (t m i j) -> p m t i j", t=PACK, i=2, j=PACK)[:, :, :, :, 2 * u : 2 * u + 2]
            nc.vector.tensor_copy(w1_dst, w1_raw[u][:].rearrange("p j (m i t) -> p m t i j", i=2, t=PACK))
        w1_codes = sb("y_codes", [P, H], U32)
        w1_scales = sb("y_scales", [P, H], U8)
        for v in range(2):
            quantise_w(w1_codes, w1_scales, w1b, v)
        y_ps = [psum.tile([P, S], F32, name="bank%d" % (PACK + t))[:] for t in range(PACK)]
        product(y_ps, w1_codes, w1_scales, x1_w, x1_s)

        dg_s = sb("dg_s", [P, H], U8, tag="w1_raw1")
        nc.vector.tensor_copy(dg_s[:], ds_tab[:].indirect(k1_t[:]))
        for r in range(4):
            nc.sync.dma_start(ds_placed[r:P:32, :].bitcast(I32), dg_s[16 * (r // 2) + r % 2 : P : 32, :].bitcast(I32))

        g2.append(sb("g2_3", [P, S], F32, tag="w1b"))
        nc.vector.tensor_copy(g2[PACK - 1][:], d[PACK - 1][:].indirect(n2_t[:]))

        for t in range(PACK + 1):
            if t < PACK:
                nc.scalar.copy(y[t][:, :S], y_ps[t])
            if t > 0:
                nc.scalar.activation(g1[:, t - 1, :], y[t - 1][:].indirect(n1_t[:]), ACT.Copy, scale=-0.5)

        dg_w = sb("dg_w", [P, H], U32)
        nc.vector.tensor_copy(dg_w[:], dw_tab[:].indirect(k1_t[:]))

        g3 = [sb("g3_0", [P, PACK, HALF], F32, tag="y_codes"), sb("g3_1", [P, PACK, HALF], F32, tag="y_scales")]
        for h in range(2):
            for t in range(PACK):
                nc.scalar.activation(g3[h][:, t, :], d[t][:].indirect(half_of(n3_t, h)), ACT.Copy)

        diff = sb("a", [P, PACK, S], F32, tag="dw_tab")
        upper = sb("m", [P, PACK, S], F32)
        for t in range(PACK + 1):
            if t < PACK:
                nc.vector.tensor_tensor(diff[:, t, :], g1[:, t, :], y[t][:, :S], ALU.add)
            if t > 0:
                nc.vector.tensor_tensor(upper[:, t - 1, :], diff[:, t - 1, :], g2[t - 1][:], ALU.min)

        gs_b = gs4[:].rearrange("p (a t b) -> p a t b", a=1, b=1).to_broadcast([P, HALF // 4, PACK, 4])
        clamped = [sb("c0", [P, PACK, HALF], F32), sb("c1", [P, PACK, HALF], F32, tag="dw_tab")]

        def clamp(h, u):
            pair = slice(2 * u, 2 * u + 2)
            nc.vector.tensor_tensor(clamped[h][:, pair, :], upper[:, pair, places(h)], g3[h][:, pair, :], ALU.max)

        def weigh(h):
            zb = sb("zb%d" % h, [P, HALF * PACK], BF16)
            nc.vector.tensor_tensor(
                zb[:].rearrange("p (c i t) -> p c t i", i=4, t=PACK),
                clamped[h][:].rearrange("p t (c i) -> p c t i", i=4), gs_b, ALU.mult)
            return zb

        def coded_layer(h, zb):
            z_w = sb("z_w%d" % h, [P, HALF], U32)
            z_s = sb("z_s%d" % h, [P, HALF], U8)
            nc.vector.quantize_mx(out=z_w[:].bitcast(FP8X4), scales=z_s[:], in_=zb[:])
            outs = [
                psum.tile([P, HALF], F32, name="h%d_%d" % (h, b), tag="bank%d" % (BLOCKS * h + b))[:]
                for b in range(BLOCKS)
            ]
            product(outs, dg_w, ds_placed, z_w, z_s)
            return outs

        clamp(0, 0)
        clamp(0, 1)
        clamp(1, 0)
        zb0 = weigh(0)
        clamp(1, 1)
        h_first = coded_layer(0, zb0)
        zb1 = weigh(1)
        h_second = coded_layer(1, zb1)

        ex_copy = sb("exc", [P, BLOCKS, S], F32)
        for b in range(BLOCKS):
            nc.scalar.activation(ex[b][:, places(0)], h_first[b], ACT.Exp, scale=EXP_SCALE)
            nc.vector.tensor_copy(ex_copy[:, b, places(0)], ex[b][:, places(0)])
        g5 = sb("g5", [P, BLOCKS, S], F32)
        sums = [sb("nd%d" % b, [P, 2, S], F32) for b in range(BLOCKS)]

        def numerator(b, cols, offsets):
            nc.vector.tensor_tensor(sums[b][:, 0, cols], ex[b][:].indirect(offsets), ex_copy[:, b, cols], ALU.add)

        for b in range(BLOCKS + 1):
            if b < BLOCKS:
                nc.scalar.activation(ex[b][:, places(1)], h_second[b], ACT.Exp, scale=EXP_SCALE)
                if b == 0:
                    numerator(0, places(0), half_of(n4_t, 0))
                nc.vector.tensor_copy(ex_copy[:, b, places(1)], ex[b][:, places(1)])
            if b > 0:
                prev = b - 1
                nc.scalar.activation(g5[:, prev, :], ex[prev][:].indirect(n5_t[:]), ACT.Copy)
                if prev == 0:
                    numerator(0, places(1), half_of(n4_t, 1))
                else:
                    numerator(prev, slice(0, S), n4_t[:])
                nc.vector.tensor_tensor(sums[prev][:, 1, :], ex[prev][:].indirect(n6_t[:]), g5[:, prev, :], ALU.add)

        for b in range(BLOCKS):
            logs = sb("ln%d" % b, [P, 2, S], F32)
            res = sb("res%d" % b, [P, S], F32)
            for cols in [slice(0, S)] if b < BLOCKS - 1 else [places(0), places(1)]:
                nc.scalar.activation(logs[:, :, cols], sums[b][:, :, cols], ACT.Ln)
                nc.vector.tensor_tensor(res[:, cols], logs[:, 0, cols], logs[:, 1, cols], ALU.subtract)
                nc.sync.dma_start(out[b * P : (b + 1) * P, cols], res[:, cols])
